import numpy as np
import ml_dtypes


def mxq(x, axis, fmt="e4m3"):
    dtype, down = {"e4m3": (ml_dtypes.float8_e4m3fn, 7), "e5m2": (ml_dtypes.float8_e5m2, 14)}[fmt]
    v = np.moveaxis(np.asarray(x, np.float32).astype(ml_dtypes.bfloat16).astype(np.float64), axis, -1)
    blocks = v.reshape(v.shape[:-1] + (-1, 32))
    amax = np.abs(blocks).max(-1, keepdims=True)
    byte = np.maximum(np.where(amax > 0, np.frexp(amax)[1] - 1 + 127, 0) - down, 1)
    scale = np.exp2(byte - 127.0)
    codes = (blocks / scale).astype(np.float32).astype(dtype).astype(np.float64)
    return np.moveaxis((codes * scale).reshape(v.shape), -1, axis)


WIDE = False


def mx_kscale(k):
    if not WIDE:
        return np.ones(k)
    levels = np.array([10, -10, 5, -5, 0])
    if k % 512:
        return np.exp2(np.random.permutation(np.resize(levels, k // 32))).repeat(32)
    a = np.empty((k // 512, 16))
    for p in range(k // 512):
        a[p, :8] = np.random.permutation(np.resize(levels, 8))
        for g in range(8):
            far = levels[np.abs(levels - a[p, g]) >= 10]
            a[p, g + 8] = far[np.random.randint(len(far))]
    return np.exp2(a.ravel()).repeat(32)


def f64(x):
    return np.asarray(x).astype(np.float64)


def striped(idx):
    return np.tile(np.asarray(idx).reshape(-1, 16).T, (8, 1)).astype(np.uint16)


def unstriped(offs):
    return offs[:16].T.reshape(-1).astype(np.int64)


def striped8(idx):
    return np.asarray(idx).reshape(8, -1, 16).transpose(0, 2, 1).reshape(128, -1).astype(np.uint16)


def unstriped8(offs):
    return offs.reshape(8, 16, -1).transpose(0, 2, 1).reshape(8, -1).astype(np.int64)


def pick8(x, idx, run):
    r = np.arange(len(x))
    return x[r[:, None], idx[r % (8 * run) // run]]


E2M1 = np.array([0.0, 0.5, 1.0, 1.5, 2.0, 3.0, 4.0, 6.0, -0.0, -0.5, -1.0, -1.5, -2.0, -3.0, -4.0, -6.0])


def pack_weight(w, fmt):
    k, n = w.shape
    w = f64(np.asarray(w, np.float32).astype(ml_dtypes.bfloat16)).reshape(k // 32, 32, n)
    amax = np.abs(w).max(1)
    if fmt == "e4m3":
        byte = np.frexp(amax)[1] - 1 + 127 - 7
    else:
        mant, ex = np.frexp(amax / 6.0)
        byte = np.where(mant > 0.5, ex, ex - 1) + 127
    byte = np.clip(np.where(amax > 0, byte, 1), 1, 254)
    scaled = (w * np.exp2(127.0 - byte)[:, None, :]).reshape(k, n).astype(np.float32)
    by_word = np.ascontiguousarray(scaled.reshape(k // 512, 128, 4, n).transpose(0, 1, 3, 2))
    if fmt == "e4m3":
        words = by_word.astype(ml_dtypes.float8_e4m3fn).view(np.uint8)
    else:
        c = by_word.astype(ml_dtypes.float4_e2m1fn).view(np.uint8) & 0xF
        words = (c[..., 0::2] | (c[..., 1::2] << 4)).reshape(k // 512, 128, 2 * n)
    return np.ascontiguousarray(words), np.ascontiguousarray(byte.astype(np.uint8).reshape(k // 512, 16, n))


def unpack_weight(words, scales, fmt):
    g, _, n = scales.shape
    words = np.ascontiguousarray(words).reshape(g, 128, n, -1)
    if fmt == "e4m3":
        vals = words.view(ml_dtypes.float8_e4m3fn).astype(np.float64)
    else:
        nib = np.empty((g, 128, n, 4), np.uint8)
        nib[..., 0::2] = words & 0xF
        nib[..., 1::2] = words >> 4
        vals = E2M1[nib]
    vals = vals * np.repeat(np.exp2(scales.astype(np.float64) - 127.0), 8, axis=1)[..., None]
    return vals.transpose(0, 1, 3, 2).reshape(g * 512, n)


K, R, F, T, J, M, G = 512, 128, 512, 2048, 512, 256, 32


def setup_inputs():
    n = np.random.standard_normal
    idx = np.random.permutation(T)[:J]
    idx2 = np.stack([np.random.permutation(J)[:M] for _ in range(8)])
    fk = mx_kscale(K)
    ff = mx_kscale(F)
    tabp = pack_weight(n((K, T)) / fk[:, None], "e2m1")
    dtabp = pack_weight(n((K, T)) / fk[:, None], "e2m1")
    return {
        "tab_words": tabp[0],
        "tab_scales": tabp[1],
        "w1": (n((K, R)) * 1 / np.sqrt(K) * fk[:, None]).astype(np.float32),
        "temper": (np.random.uniform(0.5, 1.5, (R, 1))).astype(np.float32),
        "pw": (np.random.uniform(0.5, 1.5, (1, M))).astype(np.float32),
        "wo": (n((F, R)) * 1 / np.sqrt(F) * ff[:, None]).astype(np.float32),
        "dy": (n((F, M)) / ff[:, None]).astype(np.float32),
        "dtab_words": dtabp[0],
        "dtab_scales": dtabp[1],
        "og": (np.random.uniform(0.7, 2.0, (R, 1))).astype(np.float32),
        "base": (0.3 * n((R, J))).astype(np.float32),
        "offs": striped(idx),
        "offs2": striped8(idx2),
    }


def reference(tab_words, tab_scales, w1, temper, pw, wo, dy, dtab_words, dtab_scales, og, base, offs, offs2):
    idx = unstriped(offs)
    idx2 = unstriped8(offs2)
    tabu = unpack_weight(tab_words, tab_scales, "e2m1")
    dtabu = unpack_weight(dtab_words, dtab_scales, "e2m1")
    w1q = mxq(f64(w1), 0, "e4m3")
    tabidxg = tabu[:, idx]
    a = w1q.T @ tabidxg
    dtabidxg = dtabu[:, idx]
    ta = w1q.T @ dtabidxg
    p1 = np.exp(a * f64(temper))
    s = pick8(p1, idx2, 16) * f64(pw)
    z1 = s.reshape(R, G, M // G).sum(axis=2)
    zr = np.repeat(z1, M // G, axis=1)
    woq = mxq(f64(wo), 0, "e4m3")
    dyq = mxq(f64(dy), 0, "e4m3")
    c0 = woq.T @ dyq
    dzr = c0 / (s / zr * 8.0 + 1.0) * 8.0 * s / np.square(zr) * (-1.0)
    dz1 = dzr.reshape(R, G, M // G).sum(axis=2)
    r1 = np.repeat(dz1, M // G, axis=1)
    ds = c0 / (s / zr * 8.0 + 1.0) * 8.0 / zr + r1
    e2 = ds * f64(pw)
    s2 = np.zeros((R, J))
    s2[np.arange(R)[:, None], idx2[np.arange(R) % 128 // 16]] = e2
    xp1 = ta * f64(temper) * p1
    xs = pick8(xp1, idx2, 16) * f64(pw)
    xz1 = xs.reshape(R, G, M // G).sum(axis=2)
    xzr = np.repeat(xz1, M // G, axis=1)
    xdzr = ((xs - xzr * s / zr) / zr * 8.0 * c0 / np.square(s / zr * 8.0 + 1.0) * (-1.0) * 8.0 * s + xs * c0 / (s / zr * 8.0 + 1.0) * 8.0 - xzr * zr * 2.0 * c0 / (s / zr * 8.0 + 1.0) * 8.0 * s / np.square(zr)) / np.square(zr) * (-1.0)
    xdz1 = xdzr.reshape(R, G, M // G).sum(axis=2)
    xr1 = np.repeat(xdz1, M // G, axis=1)
    xds = ((xs - xzr * s / zr) / zr * 8.0 * c0 / np.square(s / zr * 8.0 + 1.0) * (-1.0) * 8.0 - xzr * c0 / (s / zr * 8.0 + 1.0) * 8.0 / zr) / zr + xr1
    xe2 = xds * f64(pw)
    xs2 = np.zeros((R, J))
    xs2[np.arange(R)[:, None], idx2[np.arange(R) % 128 // 16]] = xe2
    xda = (xs2 * p1 + xp1 * s2) * f64(temper)
    y = xda * f64(og) + f64(base)
    return y

@@ -1,0 +1,194 @@
+from contextlib import ExitStack
+
+import concourse.mybir as mybir
+from concourse.masks import make_identity
+
+K, R, F, T, J, M, G = 512, 128, 512, 2048, 512, 256, 32
+FLOPS = 2 * K * R * J * 2 + 2 * F * R * M
+
+F32 = mybir.dt.float32
+BF16 = mybir.dt.bfloat16
+I32 = mybir.dt.int32
+U32 = mybir.dt.uint32
+U16 = mybir.dt.uint16
+U8 = mybir.dt.uint8
+FP8X4 = mybir.dt.float8_e4m3fn_x4
+FP4X4 = mybir.dt.float4_e2m1fn_x4
+ALU = mybir.AluOpType
+ACT = mybir.ActivationFunctionType
+AXIS_X = mybir.AxisListType.X
+
+P = 128
+PACK = 4
+GROUP = M // G
+
+
+def tile_attend_hvcpickshares_kernel(
+    tc, tab_words, tab_scales, w1, temper, pw, wo, dy, dtab_words, dtab_scales, og, base, offs, offs2, out
+):
+    nc = tc.nc
+    with ExitStack() as ctx:
+        sb = ctx.enter_context(tc.tile_pool(name="sb", bufs=1))
+        reuse = ctx.enter_context(tc.tile_pool(name="reuse", bufs=1))
+        ps = ctx.enter_context(tc.psum_pool(name="ps", bufs=1))
+
+        def tile(name, shape, dtype, tag=None):
+            return sb.tile(shape, dtype, name=name, tag=tag or name, align_bytes=64)
+
+        def by_group(ap):
+            return ap.rearrange("p (g i) -> p g i", i=GROUP)
+
+        def spread(per_group):
+            return per_group.unsqueeze(2).to_broadcast([P, G, GROUP])
+
+        offs_t = tile("offs_t", [P, J // 16], U16)
+        offs2_t = tile("offs2_t", [P, M // 16], U16)
+        tabw = tile("tabw", [P, T], U16)
+        dtabw = tile("dtabw", [P, T], U16)
+        dy_raw = tile("dy_raw", [P, PACK, M], F32)
+        wo_raw = tile("wo_raw", [P, PACK, R], F32)
+        base_t = tile("base_t", [P, J], F32)
+        pw_col = tile("pw_col", [P, 2], F32)
+        og_t = tile("og_t", [P, 1], F32)
+        temper_in = reuse.tile([P, 32], F32, name="temper_in", offset=3008)
+        temper_t = tile("temper_t", [P, 1], F32)
+        tabs = tile("tabs", [P, T], U8)
+        dtabs = tile("dtabs", [P, T], U8)
+        w1_raw = tile("w1_raw", [P, PACK, R], F32)
+        ident = tile("ident", [P, P], F32)
+        window = tile("window", [P, J], F32)
+
+        def load_scales(queue, plane, scales):
+            for quad in range(4):
+                queue.dma_start(
+                    out=plane[32 * quad : 32 * quad + 4, :].bitcast(I32),
+                    in_=scales[0, 4 * quad : 4 * quad + 4, :].bitcast(I32),
+                )
+
+        nc.vector.memset(tabs[:].bitcast(I32), 0)
+        nc.gpsimd.memset(dtabs[:].bitcast(I32), 0)
+        nc.vector.memset(window[:], 0.0)
+        make_identity(nc, ident[:])
+
+        nc.sync.dma_start(offs_t[:], offs)
+        nc.sync.dma_start(out=tabw[:].bitcast(I32), in_=tab_words[0].bitcast(I32))
+        load_scales(nc.sync, tabs, tab_scales)
+        nc.sync.dma_start(out=w1_raw[:], in_=w1.rearrange("(p j) r -> p j r", j=PACK))
+        nc.sync.dma_start(out=dtabw[:].bitcast(I32), in_=dtab_words[0].bitcast(I32))
+        nc.sync.dma_start(out=temper_in[:, 0:1], in_=temper)
+        nc.sync.dma_start(out=pw_col[:], in_=pw.rearrange("o (p c) -> (o p) c", c=2))
+        load_scales(nc.sync, dtabs, dtab_scales)
+        nc.sync.dma_start(offs2_t[:], offs2)
+        nc.sync.dma_start(out=dy_raw[:], in_=dy.rearrange("(p j) m -> p j m", j=PACK))
+        nc.sync.dma_start(out=wo_raw[:], in_=wo.rearrange("(p j) r -> p j r", j=PACK))
+        nc.sync.dma_start(out=og_t[:], in_=og)
+        nc.sync.dma_start(out=base_t[:], in_=base)
+        nc.gpsimd.tensor_copy(out=temper_t[:], in_=temper_in[:, 0:1])
+
+        def interleave(grouped, raw):
+            nc.scalar.copy(out=grouped[:], in_=raw[:].rearrange("p j w -> p w j"))
+            return grouped
+
+        def quantize(name, grouped, width):
+            codes = tile(name + "_codes", [P, width], U32)
+            scales = tile(name + "_scales", [P, width], U8)
+            nc.vector.quantize_mx(
+                out=codes[:].bitcast(FP8X4), scales=scales[:], in_=grouped[:].rearrange("p w j -> p (w j)")
+            )
+            return codes, scales
+
+        def gather(picked, table):
+            nc.vector.tensor_copy(picked[:], table[:].indirect(offs_t[:]))
+            return picked
+
+        def product(name, lhs, rhs_codes, rhs_scales, width):
+            bank = ps.tile([P, width], F32, name=name)
+            nc.tensor.matmul_mx(
+                out=bank[:], lhsT=lhs[0][:].bitcast(FP8X4), lhsT_scale=lhs[1][:],
+                rhs=rhs_codes, rhs_scale=rhs_scales, start=True, stop=True,
+            )
+            return bank
+
+        w1_bf = interleave(reuse.tile([P, R, PACK], BF16, name="w1_bf", offset=0, align_bytes=64), w1_raw)
+        tab_w = gather(tile("tab_w", [P, J], U16), tabw)
+        tab_s = gather(tile("tab_s", [P, J], U8), tabs)
+        w1_q = quantize("w1", w1_bf, R)
+        a = product("a", w1_q, tab_w[:].bitcast(FP4X4), tab_s[:], J)
+        p1 = tile("p1", [P, J], F32)
+        nc.scalar.activation(out=p1[:], in_=a[:], func=ACT.Exp, scale=temper_in[:, 0:1])
+        dtab_w = gather(reuse.tile([P, J], U16, name="dtab_w", offset=J, align_bytes=64), dtabw)
+        dtab_s = gather(reuse.tile([P, J], U8, name="dtab_s", offset=0, align_bytes=64), dtabs)
+        ta = product("ta", w1_q, dtab_w[:].bitcast(FP4X4), dtab_s[:], J)
+
+        pw_bank = ps.tile([P, 2, P], F32, name="pw_bank")
+        for c in range(2):
+            nc.tensor.transpose(pw_bank[:, c, :], pw_col[:, c : c + 1].to_broadcast([P, P]), ident[:])
+        pw_row = tile("pw_row", [P, M], F32, tag="w1_raw")
+        nc.scalar.copy(out=pw_row[:].rearrange("p (j c) -> p j c", c=2), in_=pw_bank[:].rearrange("p c j -> p j c"))
+
+        dy_bf = interleave(reuse.tile([P, M, PACK], BF16, name="dy_bf", offset=3072, align_bytes=64), dy_raw)
+        wo_bf = interleave(reuse.tile([P, R, PACK], BF16, name="wo_bf", offset=2048, align_bytes=64), wo_raw)
+
+        def picks(name):
+            return tile(name, [P, M], F32)
+
+        def group_sum(name, values):
+            sums = tile(name, [P, G], F32)
+            nc.vector.tensor_reduce(out=sums[:], in_=by_group(values[:]), axis=AXIS_X, op=ALU.add)
+            return sums
+
+        def product2(name, left, right, op=ALU.mult):
+            result = picks(name)
+            nc.vector.tensor_tensor(by_group(result[:]), left, right, op)
+            return result
+
+        def fused(name, left, scalar, op0, right):
+            result = picks(name)
+            nc.vector.scalar_tensor_tensor(
+                out=by_group(result[:]), in0=left, scalar=scalar, in1=right, op0=op0, op1=ALU.mult
+            )
+            return result
+
+        s = picks("s")
+        nc.vector.tensor_tensor(s[:], p1[:].indirect(offs2_t[:]), pw_row[:], ALU.mult)
+        xp1 = tile("xp1", [P, J], F32)
+        nc.vector.scalar_tensor_tensor(
+            out=xp1[:], in0=ta[:], scalar=temper_t[:], in1=p1[:], op0=ALU.mult, op1=ALU.mult
+        )
+        z = group_sum("z", s)
+        dy_q = quantize("dy", dy_bf, M)
+        rz = tile("rz", [P, G], F32)
+        nc.vector.reciprocal(out=rz[:], in_=z[:])
+        wo_q = quantize("wo", wo_bf, R)
+        c0 = product("c0", wo_q, dy_q[0][:].bitcast(FP8X4), dy_q[1][:], M)
+        u = product2("u", by_group(s[:]), spread(rz[:]))
+
+        root = picks("root")
+        nc.scalar.activation(out=root[:], in_=u[:], func=ACT.Abs_reciprocal_sqrt, scale=8.0, bias=1.0)
+        q = picks("q")
+        nc.scalar.activation(out=q[:], in_=root[:], func=ACT.Square)
+        q2 = picks("q2")
+        nc.scalar.activation(out=q2[:], in_=q[:], func=ACT.Square)
+
+        xs = reuse.tile([P, M], F32, name="xs", offset=2048)
+        nc.vector.tensor_tensor(xs[:], xp1[:].indirect(offs2_t[:]), pw_row[:], ALU.mult)
+        cz = fused("cz", by_group(c0[:]), og_t[:], ALU.mult, spread(rz[:]))
+        xz = group_sum("xz", xs)
+        nb = fused("nb", by_group(q[:]), 1.0, ALU.subtract, by_group(cz[:]))
+        y = product2("y", by_group(u[:]), spread(xz[:]))
+        e = fused("e", by_group(q2[:]), 8.0, ALU.mult, by_group(cz[:]))
+        n = product2("n", by_group(xs[:]), by_group(y[:]), ALU.subtract)
+        ns = group_sum("ns", nb)
+        en = fused("en", by_group(e[:]), temper_t[:], ALU.mult, by_group(n[:]))
+        f = product2("f", by_group(e[:]), spread(ns[:]), ALU.add)
+        ens = group_sum("ens", en)
+        g = fused("g", by_group(f[:]), temper_t[:], ALU.mult, by_group(n[:]))
+        h = fused("h", by_group(u[:]), -1.0, ALU.mult, spread(ens[:]))
+        nc.vector.tensor_tensor(window[:].indirect(offs2_t[:]), g[:], h[:], ALU.add)
+
+        res = tile("res", [P, J], F32)
+        half = J // 2
+        for part, queue in enumerate((nc.sync, nc.scalar)):
+            cols = slice(part * half, (part + 1) * half)
+            nc.vector.tensor_tensor(res[:, cols], window[:, cols], base_t[:, cols], ALU.add)
+            queue.dma_start(out=out[:, cols], in_=res[:, cols])

@@ -50,7 +50,7 @@ def tile_attend_hvcpickshares_kernel(
         base_t = tile("base_t", [P, J], F32)
         pw_col = tile("pw_col", [P, 2], F32)
         og_t = tile("og_t", [P, 1], F32)
-        temper_in = reuse.tile([P, 32], F32, name="temper_in", offset=3008)
+        temper_in = reuse.tile([P, 32], F32, name="temper_in", offset=960)
         temper_t = tile("temper_t", [P, 1], F32)
         tabs = tile("tabs", [P, T], U8)
         dtabs = tile("dtabs", [P, T], U8)
@@ -78,8 +78,8 @@ def tile_attend_hvcpickshares_kernel(
         nc.sync.dma_start(out=temper_in[:, 0:1], in_=temper)
         nc.sync.dma_start(out=pw_col[:], in_=pw.rearrange("o (p c) -> (o p) c", c=2))
         load_scales(nc.sync, dtabs, dtab_scales)
-        nc.sync.dma_start(offs2_t[:], offs2)
         nc.sync.dma_start(out=dy_raw[:], in_=dy.rearrange("(p j) m -> p j m", j=PACK))
+        nc.sync.dma_start(offs2_t[:], offs2)
         nc.sync.dma_start(out=wo_raw[:], in_=wo.rearrange("(p j) r -> p j r", j=PACK))
         nc.sync.dma_start(out=og_t[:], in_=og)
         nc.sync.dma_start(out=base_t[:], in_=base)
@@ -109,15 +109,15 @@ def tile_attend_hvcpickshares_kernel(
             )
             return bank
 
-        w1_bf = interleave(reuse.tile([P, R, PACK], BF16, name="w1_bf", offset=0, align_bytes=64), w1_raw)
+        w1_bf = interleave(tile("w1_bf", [P, R, PACK], BF16), w1_raw)
         tab_w = gather(tile("tab_w", [P, J], U16), tabw)
         tab_s = gather(tile("tab_s", [P, J], U8), tabs)
         w1_q = quantize("w1", w1_bf, R)
         a = product("a", w1_q, tab_w[:].bitcast(FP4X4), tab_s[:], J)
         p1 = tile("p1", [P, J], F32)
         nc.scalar.activation(out=p1[:], in_=a[:], func=ACT.Exp, scale=temper_in[:, 0:1])
-        dtab_w = gather(reuse.tile([P, J], U16, name="dtab_w", offset=J, align_bytes=64), dtabw)
-        dtab_s = gather(reuse.tile([P, J], U8, name="dtab_s", offset=0, align_bytes=64), dtabs)
+        dtab_w = gather(tile("dtab_w", [P, J], U16), dtabw)
+        dtab_s = gather(tile("dtab_s", [P, J], U8), dtabs)
         ta = product("ta", w1_q, dtab_w[:].bitcast(FP4X4), dtab_s[:], J)
 
         pw_bank = ps.tile([P, 2, P], F32, name="pw_bank")
@@ -125,9 +125,14 @@ def tile_attend_hvcpickshares_kernel(
             nc.tensor.transpose(pw_bank[:, c, :], pw_col[:, c : c + 1].to_broadcast([P, P]), ident[:])
         pw_row = tile("pw_row", [P, M], F32, tag="w1_raw")
         nc.scalar.copy(out=pw_row[:].rearrange("p (j c) -> p j c", c=2), in_=pw_bank[:].rearrange("p c j -> p j c"))
+        pw_temper = tile("pw_temper", [P, M], F32)
+        nc.scalar.activation(
+            out=pw_temper[:].rearrange("p (j c) -> p j c", c=2), in_=pw_bank[:].rearrange("p c j -> p j c"),
+            func=ACT.Copy, scale=temper_in[:, 0:1],
+        )
 
-        dy_bf = interleave(reuse.tile([P, M, PACK], BF16, name="dy_bf", offset=3072, align_bytes=64), dy_raw)
-        wo_bf = interleave(reuse.tile([P, R, PACK], BF16, name="wo_bf", offset=2048, align_bytes=64), wo_raw)
+        dy_bf = interleave(reuse.tile([P, M, PACK], BF16, name="dy_bf", offset=1024, align_bytes=64), dy_raw)
+        wo_bf = interleave(reuse.tile([P, R, PACK], BF16, name="wo_bf", offset=0, align_bytes=64), wo_raw)
 
         def picks(name):
             return tile(name, [P, M], F32)
@@ -151,7 +156,7 @@ def tile_attend_hvcpickshares_kernel(
 
         s = picks("s")
         nc.vector.tensor_tensor(s[:], p1[:].indirect(offs2_t[:]), pw_row[:], ALU.mult)
-        xp1 = tile("xp1", [P, J], F32)
+        xp1 = tile("xp1", [P, J], F32, tag="w1_raw")
         nc.vector.scalar_tensor_tensor(
             out=xp1[:], in0=ta[:], scalar=temper_t[:], in1=p1[:], op0=ALU.mult, op1=ALU.mult
         )
@@ -170,8 +175,8 @@ def tile_attend_hvcpickshares_kernel(
         q2 = picks("q2")
         nc.scalar.activation(out=q2[:], in_=q[:], func=ACT.Square)
 
-        xs = reuse.tile([P, M], F32, name="xs", offset=2048)
-        nc.vector.tensor_tensor(xs[:], xp1[:].indirect(offs2_t[:]), pw_row[:], ALU.mult)
+        xs = picks("xs")
+        nc.vector.tensor_tensor(xs[:], xp1[:].indirect(offs2_t[:]), pw_temper[:], ALU.mult)
         cz = fused("cz", by_group(c0[:]), og_t[:], ALU.mult, spread(rz[:]))
         xz = group_sum("xz", xs)
         nb = fused("nb", by_group(q[:]), 1.0, ALU.subtract, by_group(cz[:]))
@@ -179,10 +184,10 @@ def tile_attend_hvcpickshares_kernel(
         e = fused("e", by_group(q2[:]), 8.0, ALU.mult, by_group(cz[:]))
         n = product2("n", by_group(xs[:]), by_group(y[:]), ALU.subtract)
         ns = group_sum("ns", nb)
-        en = fused("en", by_group(e[:]), temper_t[:], ALU.mult, by_group(n[:]))
+        en = product2("en", by_group(e[:]), by_group(n[:]))
         f = product2("f", by_group(e[:]), spread(ns[:]), ALU.add)
         ens = group_sum("ens", en)
-        g = fused("g", by_group(f[:]), temper_t[:], ALU.mult, by_group(n[:]))
+        g = product2("g", by_group(f[:]), by_group(n[:]))
         h = fused("h", by_group(u[:]), -1.0, ALU.mult, spread(ens[:]))
         nc.vector.tensor_tensor(window[:].indirect(offs2_t[:]), g[:], h[:], ALU.add)
 

@@ -58,8 +58,8 @@ def tile_attend_hvcpickshares_kernel(
         ident = tile("ident", [P, P], F32)
         window = tile("window", [P, J], F32)
 
-        def load_scales(queue, plane, scales):
-            for quad in range(4):
+        def load_scales(queue, plane, scales, quads=range(4)):
+            for quad in quads:
                 queue.dma_start(
                     out=plane[32 * quad : 32 * quad + 4, :].bitcast(I32),
                     in_=scales[0, 4 * quad : 4 * quad + 4, :].bitcast(I32),
@@ -72,15 +72,16 @@ def tile_attend_hvcpickshares_kernel(
 
         nc.sync.dma_start(offs_t[:], offs)
         nc.sync.dma_start(out=tabw[:].bitcast(I32), in_=tab_words[0].bitcast(I32))
-        load_scales(nc.sync, tabs, tab_scales)
+        load_scales(nc.sync, tabs, tab_scales, range(1))
         nc.sync.dma_start(out=w1_raw[:], in_=w1.rearrange("(p j) r -> p j r", j=PACK))
+        load_scales(nc.sync, tabs, tab_scales, range(1, 4))
         nc.sync.dma_start(out=dtabw[:].bitcast(I32), in_=dtab_words[0].bitcast(I32))
         nc.sync.dma_start(out=temper_in[:, 0:1], in_=temper)
         nc.sync.dma_start(out=pw_col[:], in_=pw.rearrange("o (p c) -> (o p) c", c=2))
         load_scales(nc.sync, dtabs, dtab_scales)
         nc.sync.dma_start(out=dy_raw[:], in_=dy.rearrange("(p j) m -> p j m", j=PACK))
-        nc.sync.dma_start(offs2_t[:], offs2)
         nc.sync.dma_start(out=wo_raw[:], in_=wo.rearrange("(p j) r -> p j r", j=PACK))
+        nc.sync.dma_start(offs2_t[:], offs2)
         nc.sync.dma_start(out=og_t[:], in_=og)
         nc.sync.dma_start(out=base_t[:], in_=base)
         nc.gpsimd.tensor_copy(out=temper_t[:], in_=temper_in[:, 0:1])
@@ -125,14 +126,14 @@ def tile_attend_hvcpickshares_kernel(
             nc.tensor.transpose(pw_bank[:, c, :], pw_col[:, c : c + 1].to_broadcast([P, P]), ident[:])
         pw_row = tile("pw_row", [P, M], F32, tag="w1_raw")
         nc.scalar.copy(out=pw_row[:].rearrange("p (j c) -> p j c", c=2), in_=pw_bank[:].rearrange("p c j -> p j c"))
-        pw_temper = tile("pw_temper", [P, M], F32)
-        nc.scalar.activation(
-            out=pw_temper[:].rearrange("p (j c) -> p j c", c=2), in_=pw_bank[:].rearrange("p c j -> p j c"),
-            func=ACT.Copy, scale=temper_in[:, 0:1],
-        )
 
         dy_bf = interleave(reuse.tile([P, M, PACK], BF16, name="dy_bf", offset=1024, align_bytes=64), dy_raw)
         wo_bf = interleave(reuse.tile([P, R, PACK], BF16, name="wo_bf", offset=0, align_bytes=64), wo_raw)
+        pw_temper = tile("pw_temper", [P, M], F32, tag="dy_raw")
+        nc.scalar.activation(
+            out=pw_temper[:].rearrange("p (j c) -> p j c", c=2), in_=pw_bank[:].rearrange("p c j -> p j c"),
+            func=ACT.Copy, scale=temper_t[:],
+        )
 
         def picks(name):
             return tile(name, [P, M], F32)
@@ -156,12 +157,12 @@ def tile_attend_hvcpickshares_kernel(
 
         s = picks("s")
         nc.vector.tensor_tensor(s[:], p1[:].indirect(offs2_t[:]), pw_row[:], ALU.mult)
+        dy_q = quantize("dy", dy_bf, M)
+        z = group_sum("z", s)
         xp1 = tile("xp1", [P, J], F32, tag="w1_raw")
         nc.vector.scalar_tensor_tensor(
             out=xp1[:], in0=ta[:], scalar=temper_t[:], in1=p1[:], op0=ALU.mult, op1=ALU.mult
         )
-        z = group_sum("z", s)
-        dy_q = quantize("dy", dy_bf, M)
         rz = tile("rz", [P, G], F32)
         nc.vector.reciprocal(out=rz[:], in_=z[:])
         wo_q = quantize("wo", wo_bf, R)

@@ -21,6 +21,10 @@ AXIS_X = mybir.AxisListType.X
 P = 128
 PACK = 4
 GROUP = M // G
+QUADRANTS = 4
+LIST_ROWS = 16
+LINE = 4
+ALIGN = 64
 
 
 def tile_attend_hvcpickshares_kernel(
@@ -29,111 +33,120 @@ def tile_attend_hvcpickshares_kernel(
     nc = tc.nc
     with ExitStack() as ctx:
         sb = ctx.enter_context(tc.tile_pool(name="sb", bufs=1))
-        reuse = ctx.enter_context(tc.tile_pool(name="reuse", bufs=1))
+        overlap = ctx.enter_context(tc.tile_pool(name="overlap", bufs=1))
         ps = ctx.enter_context(tc.psum_pool(name="ps", bufs=1))
 
         def tile(name, shape, dtype, tag=None):
-            return sb.tile(shape, dtype, name=name, tag=tag or name, align_bytes=64)
+            return sb.tile(shape, dtype, name=name, tag=tag or name, align_bytes=ALIGN)
 
-        def by_group(ap):
-            return ap.rearrange("p (g i) -> p g i", i=GROUP)
+        def by_group(picks_ap):
+            return picks_ap.rearrange("p (g i) -> p g i", i=GROUP)
 
-        def spread(per_group):
-            return per_group.unsqueeze(2).to_broadcast([P, G, GROUP])
+        def spread(group_ap):
+            return group_ap.unsqueeze(2).to_broadcast([P, G, GROUP])
 
-        offs_t = tile("offs_t", [P, J // 16], U16)
-        offs2_t = tile("offs2_t", [P, M // 16], U16)
-        tabw = tile("tabw", [P, T], U16)
-        dtabw = tile("dtabw", [P, T], U16)
+        offs_t = tile("offs_t", [P, J // LIST_ROWS], U16)
+        offs2_t = tile("offs2_t", [P, M // LIST_ROWS], U16)
+        tab_word_table = tile("tab_word_table", [P, T], U16)
+        dtab_word_table = tile("dtab_word_table", [P, T], U16)
         dy_raw = tile("dy_raw", [P, PACK, M], F32)
         wo_raw = tile("wo_raw", [P, PACK, R], F32)
         base_t = tile("base_t", [P, J], F32)
-        pw_col = tile("pw_col", [P, 2], F32)
+        pw_pairs = tile("pw_pairs", [P, 2], F32)
         og_t = tile("og_t", [P, 1], F32)
-        temper_in = reuse.tile([P, 32], F32, name="temper_in", offset=960)
+        wo_bf_bytes = 2 * PACK * R
+        temper_in = overlap.tile([P, 2 * ALIGN // 4], F32, name="temper_in", offset=wo_bf_bytes - ALIGN)
         temper_t = tile("temper_t", [P, 1], F32)
-        tabs = tile("tabs", [P, T], U8)
-        dtabs = tile("dtabs", [P, T], U8)
+        tab_scale_table = tile("tab_scale_table", [P, T], U8)
+        dtab_scale_table = tile("dtab_scale_table", [P, T], U8)
         w1_raw = tile("w1_raw", [P, PACK, R], F32)
         ident = tile("ident", [P, P], F32)
         window = tile("window", [P, J], F32)
 
-        def load_scales(queue, plane, scales, quads=range(4)):
-            for quad in quads:
-                queue.dma_start(
-                    out=plane[32 * quad : 32 * quad + 4, :].bitcast(I32),
+        def load_scale_rows(table, scales, quadrants):
+            for quad in quadrants:
+                nc.sync.dma_start(
+                    out=table[32 * quad : 32 * quad + 4, :].bitcast(I32),
                     in_=scales[0, 4 * quad : 4 * quad + 4, :].bitcast(I32),
                 )
 
-        nc.vector.memset(tabs[:].bitcast(I32), 0)
-        nc.gpsimd.memset(dtabs[:].bitcast(I32), 0)
+        nc.vector.memset(tab_scale_table[:].bitcast(I32), 0)
+        nc.gpsimd.memset(dtab_scale_table[:].bitcast(I32), 0)
         nc.vector.memset(window[:], 0.0)
         make_identity(nc, ident[:])
 
         nc.sync.dma_start(offs_t[:], offs)
-        nc.sync.dma_start(out=tabw[:].bitcast(I32), in_=tab_words[0].bitcast(I32))
-        load_scales(nc.sync, tabs, tab_scales, range(1))
-        nc.sync.dma_start(out=w1_raw[:], in_=w1.rearrange("(p j) r -> p j r", j=PACK))
-        load_scales(nc.sync, tabs, tab_scales, range(1, 4))
-        nc.sync.dma_start(out=dtabw[:].bitcast(I32), in_=dtab_words[0].bitcast(I32))
+        nc.sync.dma_start(out=tab_word_table[:].bitcast(I32), in_=tab_words[0].bitcast(I32))
+        load_scale_rows(tab_scale_table, tab_scales, range(1))
+        nc.sync.dma_start(out=w1_raw[:], in_=w1.rearrange("(p t) r -> p t r", t=PACK))
+        load_scale_rows(tab_scale_table, tab_scales, range(1, QUADRANTS))
+        nc.sync.dma_start(out=dtab_word_table[:].bitcast(I32), in_=dtab_words[0].bitcast(I32))
         nc.sync.dma_start(out=temper_in[:, 0:1], in_=temper)
-        nc.sync.dma_start(out=pw_col[:], in_=pw.rearrange("o (p c) -> (o p) c", c=2))
-        load_scales(nc.sync, dtabs, dtab_scales)
-        nc.sync.dma_start(out=dy_raw[:], in_=dy.rearrange("(p j) m -> p j m", j=PACK))
-        nc.sync.dma_start(out=wo_raw[:], in_=wo.rearrange("(p j) r -> p j r", j=PACK))
-        nc.sync.dma_start(offs2_t[:], offs2)
+        nc.sync.dma_start(out=pw_pairs[:], in_=pw.rearrange("o (p c) -> (o p) c", c=2))
+        load_scale_rows(dtab_scale_table, dtab_scales, range(QUADRANTS))
+        nc.sync.dma_start(out=dy_raw[:], in_=dy.rearrange("(p t) m -> p t m", t=PACK))
         nc.sync.dma_start(out=og_t[:], in_=og)
+        nc.sync.dma_start(offs2_t[:], offs2)
+        nc.sync.dma_start(out=wo_raw[:], in_=wo.rearrange("(p t) r -> p t r", t=PACK))
         nc.sync.dma_start(out=base_t[:], in_=base)
         nc.gpsimd.tensor_copy(out=temper_t[:], in_=temper_in[:, 0:1])
 
         def interleave(grouped, raw):
-            nc.scalar.copy(out=grouped[:], in_=raw[:].rearrange("p j w -> p w j"))
+            nc.scalar.copy(
+                out=grouped[:].rearrange("p (c i) t -> p c t i", i=LINE),
+                in_=raw[:].rearrange("p t (c i) -> p c t i", i=LINE),
+            )
             return grouped
 
         def quantize(name, grouped, width):
             codes = tile(name + "_codes", [P, width], U32)
             scales = tile(name + "_scales", [P, width], U8)
             nc.vector.quantize_mx(
-                out=codes[:].bitcast(FP8X4), scales=scales[:], in_=grouped[:].rearrange("p w j -> p (w j)")
+                out=codes[:].bitcast(FP8X4), scales=scales[:], in_=grouped[:].rearrange("p w t -> p (w t)")
             )
             return codes, scales
 
-        def gather(picked, table):
+        def gather_columns(name, table, dtype):
+            picked = tile(name, [P, J], dtype)
             nc.vector.tensor_copy(picked[:], table[:].indirect(offs_t[:]))
             return picked
 
-        def product(name, lhs, rhs_codes, rhs_scales, width):
+        def mx_product(name, stationary, moving_codes, moving_scales, width):
             bank = ps.tile([P, width], F32, name=name)
             nc.tensor.matmul_mx(
-                out=bank[:], lhsT=lhs[0][:].bitcast(FP8X4), lhsT_scale=lhs[1][:],
-                rhs=rhs_codes, rhs_scale=rhs_scales, start=True, stop=True,
+                out=bank[:],
+                lhsT=stationary[0][:].bitcast(FP8X4),
+                lhsT_scale=stationary[1][:],
+                rhs=moving_codes,
+                rhs_scale=moving_scales,
+                start=True,
+                stop=True,
             )
             return bank
 
         w1_bf = interleave(tile("w1_bf", [P, R, PACK], BF16), w1_raw)
-        tab_w = gather(tile("tab_w", [P, J], U16), tabw)
-        tab_s = gather(tile("tab_s", [P, J], U8), tabs)
+        tab_w = gather_columns("tab_w", tab_word_table, U16)
+        tab_s = gather_columns("tab_s", tab_scale_table, U8)
         w1_q = quantize("w1", w1_bf, R)
-        a = product("a", w1_q, tab_w[:].bitcast(FP4X4), tab_s[:], J)
+        a = mx_product("a", w1_q, tab_w[:].bitcast(FP4X4), tab_s[:], J)
         p1 = tile("p1", [P, J], F32)
         nc.scalar.activation(out=p1[:], in_=a[:], func=ACT.Exp, scale=temper_in[:, 0:1])
-        dtab_w = gather(tile("dtab_w", [P, J], U16), dtabw)
-        dtab_s = gather(tile("dtab_s", [P, J], U8), dtabs)
-        ta = product("ta", w1_q, dtab_w[:].bitcast(FP4X4), dtab_s[:], J)
+        dtab_w = gather_columns("dtab_w", dtab_word_table, U16)
+        dtab_s = gather_columns("dtab_s", dtab_scale_table, U8)
+        ta = mx_product("ta", w1_q, dtab_w[:].bitcast(FP4X4), dtab_s[:], J)
 
         pw_bank = ps.tile([P, 2, P], F32, name="pw_bank")
         for c in range(2):
-            nc.tensor.transpose(pw_bank[:, c, :], pw_col[:, c : c + 1].to_broadcast([P, P]), ident[:])
+            nc.tensor.transpose(pw_bank[:, c, :], pw_pairs[:, c : c + 1].to_broadcast([P, P]), ident[:])
         pw_row = tile("pw_row", [P, M], F32, tag="w1_raw")
         nc.scalar.copy(out=pw_row[:].rearrange("p (j c) -> p j c", c=2), in_=pw_bank[:].rearrange("p c j -> p j c"))
-
-        dy_bf = interleave(reuse.tile([P, M, PACK], BF16, name="dy_bf", offset=1024, align_bytes=64), dy_raw)
-        wo_bf = interleave(reuse.tile([P, R, PACK], BF16, name="wo_bf", offset=0, align_bytes=64), wo_raw)
-        pw_temper = tile("pw_temper", [P, M], F32, tag="dy_raw")
-        nc.scalar.activation(
-            out=pw_temper[:].rearrange("p (j c) -> p j c", c=2), in_=pw_bank[:].rearrange("p c j -> p j c"),
-            func=ACT.Copy, scale=temper_t[:],
+        pw_temper = tile("pw_temper", [P, M], F32)
+        nc.gpsimd.tensor_scalar(
+            out=pw_temper[:], in0=pw_row[:], scalar1=temper_t[:], scalar2=0.0, op0=ALU.mult, op1=ALU.add
         )
+
+        dy_bf = interleave(overlap.tile([P, M, PACK], BF16, name="dy_bf", offset=wo_bf_bytes, align_bytes=ALIGN), dy_raw)
+        wo_bf = interleave(overlap.tile([P, R, PACK], BF16, name="wo_bf", offset=0, align_bytes=ALIGN), wo_raw)
 
         def picks(name):
             return tile(name, [P, M], F32)
@@ -143,58 +156,58 @@ def tile_attend_hvcpickshares_kernel(
             nc.vector.tensor_reduce(out=sums[:], in_=by_group(values[:]), axis=AXIS_X, op=ALU.add)
             return sums
 
-        def product2(name, left, right, op=ALU.mult):
+        def combine(name, left, right, op):
             result = picks(name)
             nc.vector.tensor_tensor(by_group(result[:]), left, right, op)
             return result
 
-        def fused(name, left, scalar, op0, right):
+        def scaled_product(name, left, scalar, scalar_op, right):
             result = picks(name)
             nc.vector.scalar_tensor_tensor(
-                out=by_group(result[:]), in0=left, scalar=scalar, in1=right, op0=op0, op1=ALU.mult
+                out=by_group(result[:]), in0=left, scalar=scalar, in1=right, op0=scalar_op, op1=ALU.mult
             )
             return result
 
         s = picks("s")
         nc.vector.tensor_tensor(s[:], p1[:].indirect(offs2_t[:]), pw_row[:], ALU.mult)
         dy_q = quantize("dy", dy_bf, M)
-        z = group_sum("z", s)
+        s_sum = group_sum("s_sum", s)
         xp1 = tile("xp1", [P, J], F32, tag="w1_raw")
         nc.vector.scalar_tensor_tensor(
             out=xp1[:], in0=ta[:], scalar=temper_t[:], in1=p1[:], op0=ALU.mult, op1=ALU.mult
         )
-        rz = tile("rz", [P, G], F32)
-        nc.vector.reciprocal(out=rz[:], in_=z[:])
+        inv_sum = tile("inv_sum", [P, G], F32)
+        nc.vector.reciprocal(out=inv_sum[:], in_=s_sum[:])
         wo_q = quantize("wo", wo_bf, R)
-        c0 = product("c0", wo_q, dy_q[0][:].bitcast(FP8X4), dy_q[1][:], M)
-        u = product2("u", by_group(s[:]), spread(rz[:]))
+        c0 = mx_product("c0", wo_q, dy_q[0][:].bitcast(FP8X4), dy_q[1][:], M)
+        share = combine("share", by_group(s[:]), spread(inv_sum[:]), ALU.mult)
 
         root = picks("root")
-        nc.scalar.activation(out=root[:], in_=u[:], func=ACT.Abs_reciprocal_sqrt, scale=8.0, bias=1.0)
+        nc.scalar.activation(out=root[:], in_=share[:], func=ACT.Abs_reciprocal_sqrt, scale=8.0, bias=1.0)
         q = picks("q")
         nc.scalar.activation(out=q[:], in_=root[:], func=ACT.Square)
-        q2 = picks("q2")
-        nc.scalar.activation(out=q2[:], in_=q[:], func=ACT.Square)
+        q_squared = picks("q_squared")
+        nc.scalar.activation(out=q_squared[:], in_=q[:], func=ACT.Square)
 
         xs = picks("xs")
         nc.vector.tensor_tensor(xs[:], xp1[:].indirect(offs2_t[:]), pw_temper[:], ALU.mult)
-        cz = fused("cz", by_group(c0[:]), og_t[:], ALU.mult, spread(rz[:]))
-        xz = group_sum("xz", xs)
-        nb = fused("nb", by_group(q[:]), 1.0, ALU.subtract, by_group(cz[:]))
-        y = product2("y", by_group(u[:]), spread(xz[:]))
-        e = fused("e", by_group(q2[:]), 8.0, ALU.mult, by_group(cz[:]))
-        n = product2("n", by_group(xs[:]), by_group(y[:]), ALU.subtract)
-        ns = group_sum("ns", nb)
-        en = product2("en", by_group(e[:]), by_group(n[:]))
-        f = product2("f", by_group(e[:]), spread(ns[:]), ALU.add)
-        ens = group_sum("ens", en)
-        g = product2("g", by_group(f[:]), by_group(n[:]))
-        h = fused("h", by_group(u[:]), -1.0, ALU.mult, spread(ens[:]))
-        nc.vector.tensor_tensor(window[:].indirect(offs2_t[:]), g[:], h[:], ALU.add)
+        cz = scaled_product("cz", by_group(c0[:]), og_t[:], ALU.mult, spread(inv_sum[:]))
+        xs_sum = group_sum("xs_sum", xs)
+        pull = scaled_product("pull", by_group(q[:]), 1.0, ALU.subtract, by_group(cz[:]))
+        xs_even = combine("xs_even", by_group(share[:]), spread(xs_sum[:]), ALU.mult)
+        slope = scaled_product("slope", by_group(q_squared[:]), 8.0, ALU.mult, by_group(cz[:]))
+        dev = combine("dev", by_group(xs[:]), by_group(xs_even[:]), ALU.subtract)
+        pull_sum = group_sum("pull_sum", pull)
+        slope_dev = combine("slope_dev", by_group(slope[:]), by_group(dev[:]), ALU.mult)
+        factor = combine("factor", by_group(slope[:]), spread(pull_sum[:]), ALU.add)
+        slope_dev_sum = group_sum("slope_dev_sum", slope_dev)
+        own_term = combine("own_term", by_group(factor[:]), by_group(dev[:]), ALU.mult)
+        group_term = scaled_product("group_term", by_group(share[:]), -1.0, ALU.mult, spread(slope_dev_sum[:]))
+        nc.vector.tensor_tensor(window[:].indirect(offs2_t[:]), own_term[:], group_term[:], ALU.add)
 
-        res = tile("res", [P, J], F32)
+        result_t = tile("result_t", [P, J], F32)
         half = J // 2
         for part, queue in enumerate((nc.sync, nc.scalar)):
             cols = slice(part * half, (part + 1) * half)
-            nc.vector.tensor_tensor(res[:, cols], window[:, cols], base_t[:, cols], ALU.add)
-            queue.dma_start(out=out[:, cols], in_=res[:, cols])
+            nc.vector.tensor_tensor(result_t[:, cols], window[:, cols], base_t[:, cols], ALU.add)
+            queue.dma_start(out=out[:, cols], in_=result_t[:, cols])

from contextlib import ExitStack

import concourse.mybir as mybir
from concourse.masks import make_identity

K, R, F, T, J, M, G = 512, 128, 512, 2048, 512, 256, 32
FLOPS = 2 * K * R * J * 2 + 2 * F * R * M

F32 = mybir.dt.float32
BF16 = mybir.dt.bfloat16
I32 = mybir.dt.int32
U32 = mybir.dt.uint32
U16 = mybir.dt.uint16
U8 = mybir.dt.uint8
FP8X4 = mybir.dt.float8_e4m3fn_x4
FP4X4 = mybir.dt.float4_e2m1fn_x4
ALU = mybir.AluOpType
ACT = mybir.ActivationFunctionType
AXIS_X = mybir.AxisListType.X

P = 128
PACK = 4
GROUP = M // G
QUADRANTS = 4
LIST_ROWS = 16
LINE = 4
ALIGN = 64


def tile_attend_hvcpickshares_kernel(
    tc, tab_words, tab_scales, w1, temper, pw, wo, dy, dtab_words, dtab_scales, og, base, offs, offs2, out
):
    nc = tc.nc
    with ExitStack() as ctx:
        sb = ctx.enter_context(tc.tile_pool(name="sb", bufs=1))
        overlap = ctx.enter_context(tc.tile_pool(name="overlap", bufs=1))
        ps = ctx.enter_context(tc.psum_pool(name="ps", bufs=1))

        def tile(name, shape, dtype, tag=None):
            return sb.tile(shape, dtype, name=name, tag=tag or name, align_bytes=ALIGN)

        def by_group(picks_ap):
            return picks_ap.rearrange("p (g i) -> p g i", i=GROUP)

        def spread(group_ap):
            return group_ap.unsqueeze(2).to_broadcast([P, G, GROUP])

        offs_t = tile("offs_t", [P, J // LIST_ROWS], U16)
        offs2_t = tile("offs2_t", [P, M // LIST_ROWS], U16)
        tab_word_table = tile("tab_word_table", [P, T], U16)
        dtab_word_table = tile("dtab_word_table", [P, T], U16)
        dy_raw = tile("dy_raw", [P, PACK, M], F32)
        wo_raw = tile("wo_raw", [P, PACK, R], F32)
        base_t = tile("base_t", [P, J], F32)
        pw_pairs = tile("pw_pairs", [P, 2], F32)
        og_t = tile("og_t", [P, 1], F32)
        wo_bf_bytes = 2 * PACK * R
        temper_in = overlap.tile([P, 2 * ALIGN // 4], F32, name="temper_in", offset=wo_bf_bytes - ALIGN)
        temper_t = tile("temper_t", [P, 1], F32)
        tab_scale_table = tile("tab_scale_table", [P, T], U8)
        dtab_scale_table = tile("dtab_scale_table", [P, T], U8)
        w1_raw = tile("w1_raw", [P, PACK, R], F32)
        ident = tile("ident", [P, P], F32)
        window = tile("window", [P, J], F32)

        def load_scale_rows(table, scales, quadrants):
            for quad in quadrants:
                nc.sync.dma_start(
                    out=table[32 * quad : 32 * quad + 4, :].bitcast(I32),
                    in_=scales[0, 4 * quad : 4 * quad + 4, :].bitcast(I32),
                )

        nc.vector.memset(tab_scale_table[:].bitcast(I32), 0)
        nc.gpsimd.memset(dtab_scale_table[:].bitcast(I32), 0)
        nc.vector.memset(window[:], 0.0)
        make_identity(nc, ident[:])

        nc.sync.dma_start(offs_t[:], offs)
        nc.sync.dma_start(out=tab_word_table[:].bitcast(I32), in_=tab_words[0].bitcast(I32))
        load_scale_rows(tab_scale_table, tab_scales, range(1))
        nc.sync.dma_start(out=w1_raw[:], in_=w1.rearrange("(p t) r -> p t r", t=PACK))
        load_scale_rows(tab_scale_table, tab_scales, range(1, QUADRANTS))
        nc.sync.dma_start(out=dtab_word_table[:].bitcast(I32), in_=dtab_words[0].bitcast(I32))
        nc.sync.dma_start(out=temper_in[:, 0:1], in_=temper)
        nc.sync.dma_start(out=pw_pairs[:], in_=pw.rearrange("o (p c) -> (o p) c", c=2))
        load_scale_rows(dtab_scale_table, dtab_scales, range(QUADRANTS))
        nc.sync.dma_start(out=dy_raw[:], in_=dy.rearrange("(p t) m -> p t m", t=PACK))
        nc.sync.dma_start(out=og_t[:], in_=og)
        nc.sync.dma_start(offs2_t[:], offs2)
        nc.sync.dma_start(out=wo_raw[:], in_=wo.rearrange("(p t) r -> p t r", t=PACK))
        nc.sync.dma_start(out=base_t[:], in_=base)
        nc.gpsimd.tensor_copy(out=temper_t[:], in_=temper_in[:, 0:1])

        def interleave(grouped, raw):
            nc.scalar.copy(
                out=grouped[:].rearrange("p (c i) t -> p c t i", i=LINE),
                in_=raw[:].rearrange("p t (c i) -> p c t i", i=LINE),
            )
            return grouped

        def quantize(name, grouped, width):
            codes = tile(name + "_codes", [P, width], U32)
            scales = tile(name + "_scales", [P, width], U8)
            nc.vector.quantize_mx(
                out=codes[:].bitcast(FP8X4), scales=scales[:], in_=grouped[:].rearrange("p w t -> p (w t)")
            )
            return codes, scales

        def gather_columns(name, table, dtype):
            picked = tile(name, [P, J], dtype)
            nc.vector.tensor_copy(picked[:], table[:].indirect(offs_t[:]))
            return picked

        def mx_product(name, stationary, moving_codes, moving_scales, width):
            bank = ps.tile([P, width], F32, name=name)
            nc.tensor.matmul_mx(
                out=bank[:],
                lhsT=stationary[0][:].bitcast(FP8X4),
                lhsT_scale=stationary[1][:],
                rhs=moving_codes,
                rhs_scale=moving_scales,
                start=True,
                stop=True,
            )
            return bank

        w1_bf = interleave(tile("w1_bf", [P, R, PACK], BF16), w1_raw)
        tab_w = gather_columns("tab_w", tab_word_table, U16)
        tab_s = gather_columns("tab_s", tab_scale_table, U8)
        w1_q = quantize("w1", w1_bf, R)
        a = mx_product("a", w1_q, tab_w[:].bitcast(FP4X4), tab_s[:], J)
        p1 = tile("p1", [P, J], F32)
        nc.scalar.activation(out=p1[:], in_=a[:], func=ACT.Exp, scale=temper_in[:, 0:1])
        dtab_w = gather_columns("dtab_w", dtab_word_table, U16)
        dtab_s = gather_columns("dtab_s", dtab_scale_table, U8)
        ta = mx_product("ta", w1_q, dtab_w[:].bitcast(FP4X4), dtab_s[:], J)

        pw_bank = ps.tile([P, 2, P], F32, name="pw_bank")
        for c in range(2):
            nc.tensor.transpose(pw_bank[:, c, :], pw_pairs[:, c : c + 1].to_broadcast([P, P]), ident[:])
        pw_row = tile("pw_row", [P, M], F32, tag="w1_raw")
        nc.scalar.copy(out=pw_row[:].rearrange("p (j c) -> p j c", c=2), in_=pw_bank[:].rearrange("p c j -> p j c"))
        pw_temper = tile("pw_temper", [P, M], F32)
        nc.gpsimd.tensor_scalar(
            out=pw_temper[:], in0=pw_row[:], scalar1=temper_t[:], scalar2=0.0, op0=ALU.mult, op1=ALU.add
        )

        dy_bf = interleave(overlap.tile([P, M, PACK], BF16, name="dy_bf", offset=wo_bf_bytes, align_bytes=ALIGN), dy_raw)
        wo_bf = interleave(overlap.tile([P, R, PACK], BF16, name="wo_bf", offset=0, align_bytes=ALIGN), wo_raw)

        def picks(name):
            return tile(name, [P, M], F32)

        def group_sum(name, values):
            sums = tile(name, [P, G], F32)
            nc.vector.tensor_reduce(out=sums[:], in_=by_group(values[:]), axis=AXIS_X, op=ALU.add)
            return sums

        def combine(name, left, right, op):
            result = picks(name)
            nc.vector.tensor_tensor(by_group(result[:]), left, right, op)
            return result

        def scaled_product(name, left, scalar, scalar_op, right):
            result = picks(name)
            nc.vector.scalar_tensor_tensor(
                out=by_group(result[:]), in0=left, scalar=scalar, in1=right, op0=scalar_op, op1=ALU.mult
            )
            return result

        s = picks("s")
        nc.vector.tensor_tensor(s[:], p1[:].indirect(offs2_t[:]), pw_row[:], ALU.mult)
        dy_q = quantize("dy", dy_bf, M)
        s_sum = group_sum("s_sum", s)
        xp1 = tile("xp1", [P, J], F32, tag="w1_raw")
        nc.vector.scalar_tensor_tensor(
            out=xp1[:], in0=ta[:], scalar=temper_t[:], in1=p1[:], op0=ALU.mult, op1=ALU.mult
        )
        inv_sum = tile("inv_sum", [P, G], F32)
        nc.vector.reciprocal(out=inv_sum[:], in_=s_sum[:])
        wo_q = quantize("wo", wo_bf, R)
        c0 = mx_product("c0", wo_q, dy_q[0][:].bitcast(FP8X4), dy_q[1][:], M)
        share = combine("share", by_group(s[:]), spread(inv_sum[:]), ALU.mult)

        root = picks("root")
        nc.scalar.activation(out=root[:], in_=share[:], func=ACT.Abs_reciprocal_sqrt, scale=8.0, bias=1.0)
        q = picks("q")
        nc.scalar.activation(out=q[:], in_=root[:], func=ACT.Square)
        q_squared = picks("q_squared")
        nc.scalar.activation(out=q_squared[:], in_=q[:], func=ACT.Square)

        xs = picks("xs")
        nc.vector.tensor_tensor(xs[:], xp1[:].indirect(offs2_t[:]), pw_temper[:], ALU.mult)
        cz = scaled_product("cz", by_group(c0[:]), og_t[:], ALU.mult, spread(inv_sum[:]))
        xs_sum = group_sum("xs_sum", xs)
        pull = scaled_product("pull", by_group(q[:]), 1.0, ALU.subtract, by_group(cz[:]))
        xs_even = combine("xs_even", by_group(share[:]), spread(xs_sum[:]), ALU.mult)
        slope = scaled_product("slope", by_group(q_squared[:]), 8.0, ALU.mult, by_group(cz[:]))
        dev = combine("dev", by_group(xs[:]), by_group(xs_even[:]), ALU.subtract)
        pull_sum = group_sum("pull_sum", pull)
        slope_dev = combine("slope_dev", by_group(slope[:]), by_group(dev[:]), ALU.mult)
        factor = combine("factor", by_group(slope[:]), spread(pull_sum[:]), ALU.add)
        slope_dev_sum = group_sum("slope_dev_sum", slope_dev)
        own_term = combine("own_term", by_group(factor[:]), by_group(dev[:]), ALU.mult)
        group_term = scaled_product("group_term", by_group(share[:]), -1.0, ALU.mult, spread(slope_dev_sum[:]))
        nc.vector.tensor_tensor(window[:].indirect(offs2_t[:]), own_term[:], group_term[:], ALU.add)

        result_t = tile("result_t", [P, J], F32)
        half = J // 2
        for part, queue in enumerate((nc.sync, nc.scalar)):
            cols = slice(part * half, (part + 1) * half)
            nc.vector.tensor_tensor(result_t[:, cols], window[:, cols], base_t[:, cols], ALU.add)
            queue.dma_start(out=out[:, cols], in_=result_t[:, cols])
